import numpy as np
import ml_dtypes


def mxq(x, axis, fmt="e4m3"):
    dtype, down = {"e4m3": (ml_dtypes.float8_e4m3fn, 7), "e5m2": (ml_dtypes.float8_e5m2, 14)}[fmt]
    v = np.moveaxis(np.asarray(x, np.float32).astype(ml_dtypes.bfloat16).astype(np.float64), axis, -1)
    blocks = v.reshape(v.shape[:-1] + (-1, 32))
    amax = np.abs(blocks).max(-1, keepdims=True)
    byte = np.maximum(np.where(amax > 0, np.frexp(amax)[1] - 1 + 127, 0) - down, 1)
    scale = np.exp2(byte - 127.0)
    codes = (blocks / scale).astype(np.float32).astype(dtype).astype(np.float64)
    return np.moveaxis((codes * scale).reshape(v.shape), -1, axis)


WIDE = False


def mx_kscale(k):
    if not WIDE:
        return np.ones(k)
    levels = np.array([10, -10, 5, -5, 0])
    if k % 512:
        return np.exp2(np.random.permutation(np.resize(levels, k // 32))).repeat(32)
    a = np.empty((k // 512, 16))
    for p in range(k // 512):
        a[p, :8] = np.random.permutation(np.resize(levels, 8))
        for g in range(8):
            far = levels[np.abs(levels - a[p, g]) >= 10]
            a[p, g + 8] = far[np.random.randint(len(far))]
    return np.exp2(a.ravel()).repeat(32)


def f64(x):
    return np.asarray(x).astype(np.float64)


def striped8(idx):
    return np.asarray(idx).reshape(8, -1, 16).transpose(0, 2, 1).reshape(128, -1).astype(np.uint16)


def unstriped8(offs):
    return offs.reshape(8, 16, -1).transpose(0, 2, 1).reshape(8, -1).astype(np.int64)


def pick8(x, idx, run):
    r = np.arange(len(x))
    return x[r[:, None], idx[r % (8 * run) // run]]


E2M1 = np.array([0.0, 0.5, 1.0, 1.5, 2.0, 3.0, 4.0, 6.0, -0.0, -0.5, -1.0, -1.5, -2.0, -3.0, -4.0, -6.0])


def pack_weight(w, fmt):
    k, n = w.shape
    w = f64(np.asarray(w, np.float32).astype(ml_dtypes.bfloat16)).reshape(k // 32, 32, n)
    amax = np.abs(w).max(1)
    if fmt == "e4m3":
        byte = np.frexp(amax)[1] - 1 + 127 - 7
    else:
        mant, ex = np.frexp(amax / 6.0)
        byte = np.where(mant > 0.5, ex, ex - 1) + 127
    byte = np.clip(np.where(amax > 0, byte, 1), 1, 254)
    scaled = (w * np.exp2(127.0 - byte)[:, None, :]).reshape(k, n).astype(np.float32)
    by_word = np.ascontiguousarray(scaled.reshape(k // 512, 128, 4, n).transpose(0, 1, 3, 2))
    if fmt == "e4m3":
        words = by_word.astype(ml_dtypes.float8_e4m3fn).view(np.uint8)
    else:
        c = by_word.astype(ml_dtypes.float4_e2m1fn).view(np.uint8) & 0xF
        words = (c[..., 0::2] | (c[..., 1::2] << 4)).reshape(k // 512, 128, 2 * n)
    return np.ascontiguousarray(words), np.ascontiguousarray(byte.astype(np.uint8).reshape(k // 512, 16, n))


def unpack_weight(words, scales, fmt):
    g, _, n = scales.shape
    words = np.ascontiguousarray(words).reshape(g, 128, n, -1)
    if fmt == "e4m3":
        vals = words.view(ml_dtypes.float8_e4m3fn).astype(np.float64)
    else:
        nib = np.empty((g, 128, n, 4), np.uint8)
        nib[..., 0::2] = words & 0xF
        nib[..., 1::2] = words >> 4
        vals = E2M1[nib]
    vals = vals * np.repeat(np.exp2(scales.astype(np.float64) - 127.0), 8, axis=1)[..., None]
    return vals.transpose(0, 1, 3, 2).reshape(g * 512, n)


D, T, U, X, I, J, Q = 512, 1024, 1024, 1024, 512, 256, 128


def setup_inputs():
    n = np.random.standard_normal
    idx = np.stack([np.random.permutation(T)[:I] for _ in range(8)])
    idx2 = np.stack([np.random.permutation(U)[:J] for _ in range(8)])
    idx3 = np.stack([np.random.permutation(X)[:J] for _ in range(8)])
    idx4 = np.stack([np.random.permutation(X)[:I] for _ in range(8)])
    fd = mx_kscale(D)
    keysp = pack_weight(n((D, T)) / fd[:, None], "e4m3")
    notesp = pack_weight(n((D, U)) / fd[:, None], "e2m1")
    usersp = pack_weight(n((D, X)) / fd[:, None], "e4m3")
    return {
        "query": (n((D, Q)) * 1.0 / np.sqrt(D) * fd[:, None]).astype(np.float32),
        "keys_words": keysp[0],
        "keys_scales": keysp[1],
        "notes_words": notesp[0],
        "notes_scales": notesp[1],
        "users_words": usersp[0],
        "users_scales": usersp[1],
        "offs": striped8(idx),
        "offs2": striped8(idx2),
        "offs3": striped8(idx3),
        "offs4": striped8(idx4),
    }


def reference(query, keys_words, keys_scales, notes_words, notes_scales, users_words, users_scales, offs, offs2, offs3, offs4):
    idx = unstriped8(offs)
    idx2 = unstriped8(offs2)
    idx3 = unstriped8(offs3)
    idx4 = unstriped8(offs4)
    keysu = unpack_weight(keys_words, keys_scales, "e4m3")
    notesu = unpack_weight(notes_words, notes_scales, "e2m1")
    usersu = unpack_weight(users_words, users_scales, "e4m3")
    queryq = mxq(f64(query), 0, "e4m3")
    a = queryq.T @ keysu
    b = queryq.T @ notesu
    c0 = queryq.T @ usersu
    w = pick8(a, idx, 16) * 1.25
    m2 = w.reshape(Q, J, I // J).max(axis=2)
    v = m2 + pick8(b, idx2, 16)
    f1 = np.zeros((Q, X))
    f1[np.arange(Q)[:, None], idx3[np.arange(Q) % 128 // 16]] = v
    cc = c0 - f1
    y = pick8(cc, idx4, 16) + w
    return y

@@ -1,0 +1,127 @@
+from contextlib import ExitStack
+
+import concourse.mybir as mybir
+
+D, T, I, J, Q = 512, 1024, 512, 256, 128
+FLOPS = 3 * 2 * D * Q * T
+
+F32 = mybir.dt.float32
+BF16 = mybir.dt.bfloat16
+I32 = mybir.dt.int32
+U32 = mybir.dt.uint32
+U16 = mybir.dt.uint16
+U8 = mybir.dt.uint8
+FP8X4 = mybir.dt.float8_e4m3fn_x4
+FP4X4 = mybir.dt.float4_e2m1fn_x4
+ALU = mybir.AluOpType
+COPY = mybir.ActivationFunctionType.Copy
+
+P = 128
+PACK = 4
+CHUNK = 256
+HALF = 512
+
+
+def tile_attend_pairjury_three_kernel(tc, query, keys_words, keys_scales, notes_words, notes_scales,
+                                       users_words, users_scales, offs, offs2, offs3, offs4, out):
+    nc = tc.nc
+    with ExitStack() as ctx:
+        keep = ctx.enter_context(tc.tile_pool(name="keep", bufs=1))
+        psum = ctx.enter_context(tc.psum_pool(name="psum", bufs=1))
+
+        def scale_plane(name):
+            plane = keep.tile([P, T], U8, name=name, align_bytes=64)
+            nc.vector.memset(plane[:].bitcast(I32), 0)
+            return plane
+
+        def load_scales(plane, rows):
+            for quad in range(4):
+                nc.sync.dma_start(out=plane[32 * quad:32 * quad + 4, :].bitcast(I32),
+                                  in_=rows[0, 4 * quad:4 * quad + 4, :].bitcast(I32))
+
+        def load_list(name, src):
+            lst = keep.tile(list(src.shape), U16, name=name)
+            nc.sync.dma_start(lst[:], src)
+            return lst
+
+        k_plane = scale_plane("k_plane")
+        n_plane = scale_plane("n_plane")
+        u_plane = scale_plane("u_plane")
+        f1 = keep.tile([P, T], F32, name="f1")
+        nc.vector.memset(f1[:], 0.0)
+
+        q_raw = keep.tile([P, PACK, Q], F32, name="q_raw")
+        nc.sync.dma_start(out=q_raw[:], in_=query.rearrange("(p r) q -> p r q", r=PACK))
+        load_scales(k_plane, keys_scales)
+        k_src = keys_words[0].rearrange("p n r -> p (n r)").bitcast(I32)
+        k_words = []
+        for h in range(2):
+            words = keep.tile([P, HALF], U32, name="k_words%d" % h, align_bytes=64)
+            nc.sync.dma_start(out=words[:].bitcast(I32), in_=k_src[:, h * HALF:(h + 1) * HALF])
+            k_words.append(words)
+        idx = load_list("idx", offs)
+        n_words = keep.tile([P, 2 * T], U8, name="n_words", align_bytes=64)
+        nc.sync.dma_start(out=n_words[:].bitcast(I32), in_=notes_words[0].bitcast(I32))
+        load_scales(n_plane, notes_scales)
+        idx2 = load_list("idx2", offs2)
+        u_words = keep.tile([P, T], U32, name="u_words", align_bytes=64)
+        nc.sync.dma_start(out=u_words[:].bitcast(I32),
+                          in_=users_words[0].rearrange("p n r -> p (n r)").bitcast(I32))
+        idx3 = load_list("idx3", offs3)
+        load_scales(u_plane, users_scales)
+        idx4 = load_list("idx4", offs4)
+
+        q_grouped = keep.tile([P, Q, PACK], BF16, name="q_grouped", align_bytes=64)
+        nc.vector.tensor_copy(out=q_grouped[:], in_=q_raw[:].rearrange("p r q -> p q r"))
+        q_codes = keep.tile([P, Q], U32, name="q_codes", align_bytes=64)
+        q_plane = keep.tile([P, Q], U8, name="q_plane", align_bytes=64)
+        nc.vector.quantize_mx(out=q_codes[:].bitcast(FP8X4), scales=q_plane[:],
+                              in_=q_grouped[:].rearrange("p q r -> p (q r)"))
+
+        def score(bank, words, plane):
+            nc.tensor.matmul_mx(out=bank, lhsT=q_codes[:].bitcast(FP8X4), lhsT_scale=q_plane[:],
+                                rhs=words, rhs_scale=plane, start=True, stop=True)
+
+        a = keep.tile([P, T], F32, name="a")
+        for c in range(T // CHUNK):
+            cols = slice(c * CHUNK, (c + 1) * CHUNK)
+            bank = psum.tile([P, CHUNK], F32, name="a_bank%d" % c, tag="bank%d" % c)
+            h, at = divmod(c * CHUNK, HALF)
+            score(bank[:], k_words[h][:, at:at + CHUNK].bitcast(FP8X4), k_plane[:, cols])
+            nc.vector.tensor_copy(out=a[:, cols], in_=bank[:])
+
+        b = keep.tile([P, T], F32, name="b")
+        for c in range(T // CHUNK):
+            cols = slice(c * CHUNK, (c + 1) * CHUNK)
+            bank = psum.tile([P, CHUNK], F32, name="b_bank%d" % c, tag="bank%d" % (4 + c))
+            score(bank[:], n_words[:, 2 * c * CHUNK:2 * (c + 1) * CHUNK].bitcast(FP4X4), n_plane[:, cols])
+            nc.scalar.copy(out=b[:, cols], in_=bank[:])
+
+        c_banks = []
+        for h in range(2):
+            cols = slice(h * HALF, (h + 1) * HALF)
+            bank = psum.tile([P, HALF], F32, name="c_bank%d" % h, tag="bank%d" % h)
+            score(bank[:], u_words[:, cols].bitcast(FP8X4), u_plane[:, cols])
+            c_banks.append(bank)
+
+        w = keep.tile([P, I], F32, name="w")
+        nc.vector.tensor_scalar(w[:], a[:].indirect(idx[:]), 1.25, 0.0, ALU.mult, ALU.add)
+        b_picked = keep.tile([P, J], F32, name="b_picked")
+        nc.scalar.activation(b_picked[:], b[:].indirect(idx2[:]), COPY)
+        m2 = keep.tile([P, J], F32, name="m2")
+        nc.vector.tensor_tensor(m2[:], w[:, 0:I:2], w[:, 1:I:2], ALU.max)
+        nc.vector.tensor_tensor(f1[:].indirect(idx3[:]), m2[:], b_picked[:], ALU.add)
+
+        cc = keep.tile([P, T], F32, name="cc")
+        for h in range(2):
+            cols = slice(h * HALF, (h + 1) * HALF)
+            nc.vector.tensor_tensor(cc[:, cols], c_banks[h][:], f1[:, cols], ALU.subtract)
+
+        y0 = keep.tile([P, J], F32, name="y0")
+        nc.vector.tensor_tensor(y0[:], cc[:].indirect(idx4[:, 0:16]), w[:, 0:J], ALU.add)
+        nc.sync.dma_start(out=out[:, 0:J], in_=y0[:])
+        cc_picked = keep.tile([P, J], F32, name="cc_picked")
+        nc.scalar.activation(cc_picked[:], cc[:].indirect(idx4[:, 16:32]), COPY)
+        y1 = keep.tile([P, J], F32, name="y1")
+        nc.vector.tensor_tensor(y1[:], cc_picked[:], w[:, J:I], ALU.add)
+        nc.sync.dma_start(out=out[:, J:I], in_=y1[:])

@@ -31,13 +31,11 @@ def tile_attend_pairjury_three_kernel(tc, query, keys_words, keys_scales, notes_
 
         def scale_plane(name):
             plane = keep.tile([P, T], U8, name=name, align_bytes=64)
-            nc.vector.memset(plane[:].bitcast(I32), 0)
             return plane
 
         def load_scales(plane, rows):
-            for quad in range(4):
-                nc.sync.dma_start(out=plane[32 * quad:32 * quad + 4, :].bitcast(I32),
-                                  in_=rows[0, 4 * quad:4 * quad + 4, :].bitcast(I32))
+            for r in range(4):
+                nc.sync.dma_start(out=plane[r:P:32, :].bitcast(I32), in_=rows[0, r:16:4, :].bitcast(I32))
 
         def load_list(name, src):
             lst = keep.tile(list(src.shape), U16, name=name)
@@ -50,29 +48,28 @@ def tile_attend_pairjury_three_kernel(tc, query, keys_words, keys_scales, notes_
         f1 = keep.tile([P, T], F32, name="f1")
         nc.vector.memset(f1[:], 0.0)
 
+        def load_words(name, src, dtype):
+            words = keep.tile([P, src.shape[1]], dtype, name=name, align_bytes=64)
+            nc.sync.dma_start(out=words[:].bitcast(I32), in_=src.bitcast(I32))
+            return words
+
         q_raw = keep.tile([P, PACK, Q], F32, name="q_raw")
         nc.sync.dma_start(out=q_raw[:], in_=query.rearrange("(p r) q -> p r q", r=PACK))
         load_scales(k_plane, keys_scales)
-        k_src = keys_words[0].rearrange("p n r -> p (n r)").bitcast(I32)
-        k_words = []
-        for h in range(2):
-            words = keep.tile([P, HALF], U32, name="k_words%d" % h, align_bytes=64)
-            nc.sync.dma_start(out=words[:].bitcast(I32), in_=k_src[:, h * HALF:(h + 1) * HALF])
-            k_words.append(words)
-        idx = load_list("idx", offs)
-        n_words = keep.tile([P, 2 * T], U8, name="n_words", align_bytes=64)
-        nc.sync.dma_start(out=n_words[:].bitcast(I32), in_=notes_words[0].bitcast(I32))
+        k_src = keys_words[0].rearrange("p n r -> p (n r)")
+        k_words = [load_words("k_words%d" % h, k_src[:, 4 * h * HALF:4 * (h + 1) * HALF], U8) for h in range(2)]
+        n_words = load_words("n_words", notes_words[0], U8)
         load_scales(n_plane, notes_scales)
+        idx = load_list("idx", offs)
         idx2 = load_list("idx2", offs2)
-        u_words = keep.tile([P, T], U32, name="u_words", align_bytes=64)
-        nc.sync.dma_start(out=u_words[:].bitcast(I32),
-                          in_=users_words[0].rearrange("p n r -> p (n r)").bitcast(I32))
+        u_words = load_words("u_words", users_words[0].rearrange("p n r -> p (n r)"), U8)
         idx3 = load_list("idx3", offs3)
         load_scales(u_plane, users_scales)
         idx4 = load_list("idx4", offs4)
 
         q_grouped = keep.tile([P, Q, PACK], BF16, name="q_grouped", align_bytes=64)
-        nc.vector.tensor_copy(out=q_grouped[:], in_=q_raw[:].rearrange("p r q -> p q r"))
+        nc.vector.tensor_copy(out=q_grouped[:].rearrange("p (c i) r -> p c r i", i=4),
+                              in_=q_raw[:].rearrange("p r (c i) -> p c r i", i=4))
         q_codes = keep.tile([P, Q], U32, name="q_codes", align_bytes=64)
         q_plane = keep.tile([P, Q], U8, name="q_plane", align_bytes=64)
         nc.vector.quantize_mx(out=q_codes[:].bitcast(FP8X4), scales=q_plane[:],
@@ -87,7 +84,7 @@ def tile_attend_pairjury_three_kernel(tc, query, keys_words, keys_scales, notes_
             cols = slice(c * CHUNK, (c + 1) * CHUNK)
             bank = psum.tile([P, CHUNK], F32, name="a_bank%d" % c, tag="bank%d" % c)
             h, at = divmod(c * CHUNK, HALF)
-            score(bank[:], k_words[h][:, at:at + CHUNK].bitcast(FP8X4), k_plane[:, cols])
+            score(bank[:], k_words[h][:, 4 * at:4 * (at + CHUNK)].bitcast(FP8X4), k_plane[:, cols])
             nc.vector.tensor_copy(out=a[:, cols], in_=bank[:])
 
         b = keep.tile([P, T], F32, name="b")
@@ -101,7 +98,7 @@ def tile_attend_pairjury_three_kernel(tc, query, keys_words, keys_scales, notes_
         for h in range(2):
             cols = slice(h * HALF, (h + 1) * HALF)
             bank = psum.tile([P, HALF], F32, name="c_bank%d" % h, tag="bank%d" % h)
-            score(bank[:], u_words[:, cols].bitcast(FP8X4), u_plane[:, cols])
+            score(bank[:], u_words[:, 4 * h * HALF:4 * (h + 1) * HALF].bitcast(FP8X4), u_plane[:, cols])
             c_banks.append(bank)
 
         w = keep.tile([P, I], F32, name="w")

@@ -18,7 +18,8 @@ COPY = mybir.ActivationFunctionType.Copy
 
 P = 128
 PACK = 4
-CHUNK = 256
+CHUNKS = [(0, 256), (256, 512), (512, 768), (768, 896), (896, 1024)]
+C_CHUNKS = [(0, 512), (512, 768), (768, 1024)]
 HALF = 512
 
 
@@ -67,39 +68,46 @@ def tile_attend_pairjury_three_kernel(tc, query, keys_words, keys_scales, notes_
         load_scales(u_plane, users_scales)
         idx4 = load_list("idx4", offs4)
 
-        q_grouped = keep.tile([P, Q, PACK], BF16, name="q_grouped", align_bytes=64)
-        nc.vector.tensor_copy(out=q_grouped[:].rearrange("p (c i) r -> p c r i", i=4),
-                              in_=q_raw[:].rearrange("p r (c i) -> p c r i", i=4))
         q_codes = keep.tile([P, Q], U32, name="q_codes", align_bytes=64)
         q_plane = keep.tile([P, Q], U8, name="q_plane", align_bytes=64)
-        nc.vector.quantize_mx(out=q_codes[:].bitcast(FP8X4), scales=q_plane[:],
-                              in_=q_grouped[:].rearrange("p q r -> p (q r)"))
+        q_grouped = []
+        for h in range(2):
+            grouped = keep.tile([P, Q // 2, PACK], BF16, name="q_grouped%d" % h, align_bytes=64)
+            nc.vector.tensor_copy(out=grouped[:].rearrange("p (c i) r -> p c r i", i=4),
+                                  in_=q_raw[:, :, h * 64:(h + 1) * 64].rearrange("p r (c i) -> p c r i", i=4))
+            q_grouped.append(grouped)
+        for h in range(2):
+            nc.vector.quantize_mx(out=q_codes[:, h * 64:(h + 1) * 64].bitcast(FP8X4),
+                                  scales=q_plane[:, h * 64:(h + 1) * 64],
+                                  in_=q_grouped[h][:].rearrange("p q r -> p (q r)"))
 
         def score(bank, words, plane):
             nc.tensor.matmul_mx(out=bank, lhsT=q_codes[:].bitcast(FP8X4), lhsT_scale=q_plane[:],
                                 rhs=words, rhs_scale=plane, start=True, stop=True)
 
+        def bank_for(name, n, width):
+            return psum.tile([P, width], F32, name=name, tag="bank%d" % (n % 8))
+
         a = keep.tile([P, T], F32, name="a")
-        for c in range(T // CHUNK):
-            cols = slice(c * CHUNK, (c + 1) * CHUNK)
-            bank = psum.tile([P, CHUNK], F32, name="a_bank%d" % c, tag="bank%d" % c)
-            h, at = divmod(c * CHUNK, HALF)
-            score(bank[:], k_words[h][:, 4 * at:4 * (at + CHUNK)].bitcast(FP8X4), k_plane[:, cols])
-            nc.vector.tensor_copy(out=a[:, cols], in_=bank[:])
+        for c, (lo, hi) in enumerate(CHUNKS):
+            bank = bank_for("a_bank%d" % c, c, hi - lo)
+            h, at = divmod(lo, HALF)
+            score(bank[:], k_words[h][:, 4 * at:4 * (at + hi - lo)].bitcast(FP8X4), k_plane[:, lo:hi])
+            nc.vector.tensor_copy(out=a[:, lo:hi], in_=bank[:])
 
         b = keep.tile([P, T], F32, name="b")
-        for c in range(T // CHUNK):
-            cols = slice(c * CHUNK, (c + 1) * CHUNK)
-            bank = psum.tile([P, CHUNK], F32, name="b_bank%d" % c, tag="bank%d" % (4 + c))
-            score(bank[:], n_words[:, 2 * c * CHUNK:2 * (c + 1) * CHUNK].bitcast(FP4X4), n_plane[:, cols])
-            nc.scalar.copy(out=b[:, cols], in_=bank[:])
+        for c, (lo, hi) in enumerate(CHUNKS):
+            bank = bank_for("b_bank%d" % c, len(CHUNKS) + c, hi - lo)
+            score(bank[:], n_words[:, 2 * lo:2 * hi].bitcast(FP4X4), n_plane[:, lo:hi])
+            nc.scalar.copy(out=b[:, lo:hi], in_=bank[:])
 
         c_banks = []
-        for h in range(2):
-            cols = slice(h * HALF, (h + 1) * HALF)
-            bank = psum.tile([P, HALF], F32, name="c_bank%d" % h, tag="bank%d" % h)
-            score(bank[:], u_words[:, 4 * h * HALF:4 * (h + 1) * HALF].bitcast(FP8X4), u_plane[:, cols])
+        for c, (lo, hi) in enumerate(C_CHUNKS):
+            bank = bank_for("c_bank%d" % c, 2 * len(CHUNKS) + c, hi - lo)
+            score(bank[:], u_words[:, 4 * lo:4 * hi].bitcast(FP8X4), u_plane[:, lo:hi])
             c_banks.append(bank)
+        c0_last = keep.tile([P, 256], F32, name="c0_last")
+        nc.scalar.copy(out=c0_last[:], in_=c_banks[2][:])
 
         w = keep.tile([P, I], F32, name="w")
         nc.vector.tensor_scalar(w[:], a[:].indirect(idx[:]), 1.25, 0.0, ALU.mult, ALU.add)
@@ -110,9 +118,9 @@ def tile_attend_pairjury_three_kernel(tc, query, keys_words, keys_scales, notes_
         nc.vector.tensor_tensor(f1[:].indirect(idx3[:]), m2[:], b_picked[:], ALU.add)
 
         cc = keep.tile([P, T], F32, name="cc")
-        for h in range(2):
-            cols = slice(h * HALF, (h + 1) * HALF)
-            nc.vector.tensor_tensor(cc[:, cols], c_banks[h][:], f1[:, cols], ALU.subtract)
+        nc.gpsimd.tensor_tensor(cc[:, 768:T], c0_last[:], f1[:, 768:T], ALU.subtract)
+        for c, (lo, hi) in enumerate(C_CHUNKS[:2]):
+            nc.vector.tensor_tensor(cc[:, lo:hi], c_banks[c][:], f1[:, lo:hi], ALU.subtract)
 
         y0 = keep.tile([P, J], F32, name="y0")
         nc.vector.tensor_tensor(y0[:], cc[:].indirect(idx4[:, 0:16]), w[:, 0:J], ALU.add)

from contextlib import ExitStack

import concourse.mybir as mybir

D, T, I, J, Q = 512, 1024, 512, 256, 128
FLOPS = 3 * 2 * D * Q * T

F32 = mybir.dt.float32
BF16 = mybir.dt.bfloat16
I32 = mybir.dt.int32
U32 = mybir.dt.uint32
U16 = mybir.dt.uint16
U8 = mybir.dt.uint8
FP8X4 = mybir.dt.float8_e4m3fn_x4
FP4X4 = mybir.dt.float4_e2m1fn_x4
ALU = mybir.AluOpType
COPY = mybir.ActivationFunctionType.Copy

P = 128
PACK = 4
CHUNKS = [(0, 256), (256, 512), (512, 768), (768, 896), (896, 1024)]
C_CHUNKS = [(0, 512), (512, 768), (768, 1024)]
HALF = 512


def tile_attend_pairjury_three_kernel(tc, query, keys_words, keys_scales, notes_words, notes_scales,
                                       users_words, users_scales, offs, offs2, offs3, offs4, out):
    nc = tc.nc
    with ExitStack() as ctx:
        keep = ctx.enter_context(tc.tile_pool(name="keep", bufs=1))
        psum = ctx.enter_context(tc.psum_pool(name="psum", bufs=1))

        def scale_plane(name):
            plane = keep.tile([P, T], U8, name=name, align_bytes=64)
            return plane

        def load_scales(plane, rows):
            for r in range(4):
                nc.sync.dma_start(out=plane[r:P:32, :].bitcast(I32), in_=rows[0, r:16:4, :].bitcast(I32))

        def load_list(name, src):
            lst = keep.tile(list(src.shape), U16, name=name)
            nc.sync.dma_start(lst[:], src)
            return lst

        k_plane = scale_plane("k_plane")
        n_plane = scale_plane("n_plane")
        u_plane = scale_plane("u_plane")
        f1 = keep.tile([P, T], F32, name="f1")
        nc.vector.memset(f1[:], 0.0)

        def load_words(name, src, dtype):
            words = keep.tile([P, src.shape[1]], dtype, name=name, align_bytes=64)
            nc.sync.dma_start(out=words[:].bitcast(I32), in_=src.bitcast(I32))
            return words

        q_raw = keep.tile([P, PACK, Q], F32, name="q_raw")
        nc.sync.dma_start(out=q_raw[:], in_=query.rearrange("(p r) q -> p r q", r=PACK))
        load_scales(k_plane, keys_scales)
        k_src = keys_words[0].rearrange("p n r -> p (n r)")
        k_words = [load_words("k_words%d" % h, k_src[:, 4 * h * HALF:4 * (h + 1) * HALF], U8) for h in range(2)]
        n_words = load_words("n_words", notes_words[0], U8)
        load_scales(n_plane, notes_scales)
        idx = load_list("idx", offs)
        idx2 = load_list("idx2", offs2)
        u_words = load_words("u_words", users_words[0].rearrange("p n r -> p (n r)"), U8)
        idx3 = load_list("idx3", offs3)
        load_scales(u_plane, users_scales)
        idx4 = load_list("idx4", offs4)

        q_codes = keep.tile([P, Q], U32, name="q_codes", align_bytes=64)
        q_plane = keep.tile([P, Q], U8, name="q_plane", align_bytes=64)
        q_grouped = []
        for h in range(2):
            grouped = keep.tile([P, Q // 2, PACK], BF16, name="q_grouped%d" % h, align_bytes=64)
            nc.vector.tensor_copy(out=grouped[:].rearrange("p (c i) r -> p c r i", i=4),
                                  in_=q_raw[:, :, h * 64:(h + 1) * 64].rearrange("p r (c i) -> p c r i", i=4))
            q_grouped.append(grouped)
        for h in range(2):
            nc.vector.quantize_mx(out=q_codes[:, h * 64:(h + 1) * 64].bitcast(FP8X4),
                                  scales=q_plane[:, h * 64:(h + 1) * 64],
                                  in_=q_grouped[h][:].rearrange("p q r -> p (q r)"))

        def score(bank, words, plane):
            nc.tensor.matmul_mx(out=bank, lhsT=q_codes[:].bitcast(FP8X4), lhsT_scale=q_plane[:],
                                rhs=words, rhs_scale=plane, start=True, stop=True)

        def bank_for(name, n, width):
            return psum.tile([P, width], F32, name=name, tag="bank%d" % (n % 8))

        a = keep.tile([P, T], F32, name="a")
        for c, (lo, hi) in enumerate(CHUNKS):
            bank = bank_for("a_bank%d" % c, c, hi - lo)
            h, at = divmod(lo, HALF)
            score(bank[:], k_words[h][:, 4 * at:4 * (at + hi - lo)].bitcast(FP8X4), k_plane[:, lo:hi])
            nc.vector.tensor_copy(out=a[:, lo:hi], in_=bank[:])

        b = keep.tile([P, T], F32, name="b")
        for c, (lo, hi) in enumerate(CHUNKS):
            bank = bank_for("b_bank%d" % c, len(CHUNKS) + c, hi - lo)
            score(bank[:], n_words[:, 2 * lo:2 * hi].bitcast(FP4X4), n_plane[:, lo:hi])
            nc.scalar.copy(out=b[:, lo:hi], in_=bank[:])

        c_banks = []
        for c, (lo, hi) in enumerate(C_CHUNKS):
            bank = bank_for("c_bank%d" % c, 2 * len(CHUNKS) + c, hi - lo)
            score(bank[:], u_words[:, 4 * lo:4 * hi].bitcast(FP8X4), u_plane[:, lo:hi])
            c_banks.append(bank)
        c0_last = keep.tile([P, 256], F32, name="c0_last")
        nc.scalar.copy(out=c0_last[:], in_=c_banks[2][:])

        w = keep.tile([P, I], F32, name="w")
        nc.vector.tensor_scalar(w[:], a[:].indirect(idx[:]), 1.25, 0.0, ALU.mult, ALU.add)
        b_picked = keep.tile([P, J], F32, name="b_picked")
        nc.scalar.activation(b_picked[:], b[:].indirect(idx2[:]), COPY)
        m2 = keep.tile([P, J], F32, name="m2")
        nc.vector.tensor_tensor(m2[:], w[:, 0:I:2], w[:, 1:I:2], ALU.max)
        nc.vector.tensor_tensor(f1[:].indirect(idx3[:]), m2[:], b_picked[:], ALU.add)

        cc = keep.tile([P, T], F32, name="cc")
        nc.gpsimd.tensor_tensor(cc[:, 768:T], c0_last[:], f1[:, 768:T], ALU.subtract)
        for c, (lo, hi) in enumerate(C_CHUNKS[:2]):
            nc.vector.tensor_tensor(cc[:, lo:hi], c_banks[c][:], f1[:, lo:hi], ALU.subtract)

        y0 = keep.tile([P, J], F32, name="y0")
        nc.vector.tensor_tensor(y0[:], cc[:].indirect(idx4[:, 0:16]), w[:, 0:J], ALU.add)
        nc.sync.dma_start(out=out[:, 0:J], in_=y0[:])
        cc_picked = keep.tile([P, J], F32, name="cc_picked")
        nc.scalar.activation(cc_picked[:], cc[:].indirect(idx4[:, 16:32]), COPY)
        y1 = keep.tile([P, J], F32, name="y1")
        nc.vector.tensor_tensor(y1[:], cc_picked[:], w[:, J:I], ALU.add)
        nc.sync.dma_start(out=out[:, J:I], in_=y1[:])
